import numpy as np
import ml_dtypes


def mxq(x, axis, fmt="e4m3"):
    dtype, down = {"e4m3": (ml_dtypes.float8_e4m3fn, 7), "e5m2": (ml_dtypes.float8_e5m2, 14)}[fmt]
    v = np.moveaxis(np.asarray(x, np.float32).astype(ml_dtypes.bfloat16).astype(np.float64), axis, -1)
    blocks = v.reshape(v.shape[:-1] + (-1, 32))
    amax = np.abs(blocks).max(-1, keepdims=True)
    byte = np.maximum(np.where(amax > 0, np.frexp(amax)[1] - 1 + 127, 0) - down, 1)
    scale = np.exp2(byte - 127.0)
    codes = (blocks / scale).astype(np.float32).astype(dtype).astype(np.float64)
    return np.moveaxis((codes * scale).reshape(v.shape), -1, axis)


WIDE = False


def mx_kscale(k):
    if not WIDE:
        return np.ones(k)
    levels = np.array([10, -10, 5, -5, 0])
    if k % 512:
        return np.exp2(np.random.permutation(np.resize(levels, k // 32))).repeat(32)
    a = np.empty((k // 512, 16))
    for p in range(k // 512):
        a[p, :8] = np.random.permutation(np.resize(levels, 8))
        for g in range(8):
            far = levels[np.abs(levels - a[p, g]) >= 10]
            a[p, g + 8] = far[np.random.randint(len(far))]
    return np.exp2(a.ravel()).repeat(32)


BF16 = ml_dtypes.bfloat16


def bf(x):
    return np.asarray(x, np.float32).astype(BF16)


def f64(x):
    return np.asarray(x).astype(np.float64)


B, Q, N, D, K = 2, 128, 1024, 512, 512
C2 = 2
C4 = 4


def sigmoid(v):
    return 1.0 / (1.0 + np.exp(-v))


def soft_side(center, half, coord):
    dist = np.abs(coord[None, None, :] - center[:, :, None])
    return sigmoid(8.0 * (half[:, :, None] - dist))


def draw0():
    s, r, t = mx_kscale(D), mx_kscale(D), mx_kscale(K)
    return {
        "f": bf(np.random.standard_normal((B, N, D)) * s),
        "wp": bf(np.random.standard_normal((D, K)) / np.sqrt(D) / s[:, None] / t[None, :]),
        "x": bf(np.random.standard_normal((B, Q, D)) * r),
        "wc": bf(np.random.standard_normal((D, K)) / np.sqrt(D) / r[:, None]),
        "g": bf((1.0 + 0.2 * np.random.standard_normal(K)) * t),
        "box": bf(np.random.uniform(0.2, 0.8, (B, Q, C4))),
        "pix": bf(np.random.uniform(0.0, 1.0, (N, C2))),
    }


def core(f, wp, x, wc, g, box, pix):
    p = mxq(f64(f), 2, "e4m3") @ mxq(f64(wp), 0, "e4m3")

    h = mxq(f64(x), 2, "e4m3") @ mxq(f64(wc), 0, "e4m3")
    c = np.tanh(h) * f64(g)[None, None, :]

    m = 3.0 * (mxq(c, 2, "e4m3") @ mxq(p, 2, "e4m3").transpose(0, 2, 1)) / np.sqrt(K)

    bx, px = f64(box), f64(pix)
    crop = soft_side(bx[:, :, 0], bx[:, :, 2], px[:, 0]) * soft_side(bx[:, :, 1], bx[:, :, 3], px[:, 1])

    return sigmoid(m) * crop


def e4m3fn_bytes(y):
    return np.clip(np.asarray(y, np.float64), -448.0, 448.0).astype(np.float32).astype(ml_dtypes.float8_e4m3fn).view(np.uint8)


def e4m3fn_values(b):
    return np.asarray(b, np.uint8).view(ml_dtypes.float8_e4m3fn).astype(np.float64)


def setup_inputs():
    d = draw0()
    x0 = np.asarray(d['f']).astype(np.float64)
    s = (np.max(np.abs(x0), axis=(0, 1), keepdims=True) / 448.0).astype(np.float32)
    out = {}
    for k, v in d.items():
        if k == 'f':
            out['f_bytes'] = e4m3fn_bytes(x0 / s.astype(np.float64))
            out['f_scale'] = s
        else:
            out[k] = v
    return out


def reference(f_bytes, f_scale, wp, x, wc, g, box, pix):
    return core(e4m3fn_values(f_bytes) * f_scale.astype(np.float64), wp, x, wc, g, box, pix)

@@ -1,0 +1,357 @@
+from contextlib import ExitStack
+from math import sqrt
+
+import concourse.mybir as mybir
+from concourse.masks import make_identity
+
+B, Q, N, D, K = 2, 128, 1024, 512, 512
+FLOPS = 2 * B * N * D * K + 2 * B * Q * D * K + 2 * B * Q * N * K
+
+F32 = mybir.dt.float32
+BF16 = mybir.dt.bfloat16
+U32 = mybir.dt.uint32
+U8 = mybir.dt.uint8
+FP8 = mybir.dt.float8_e4m3fn
+FP8X4 = mybir.dt.float8_e4m3fn_x4
+ACT = mybir.ActivationFunctionType
+ALU = mybir.AluOpType
+
+P = 128
+CH = 256
+CHUNKS = B * N // CH
+
+
+def tile_prototypecoefficientsoftcropmasks_kernel(
+    tc, f_bytes, f_scale, wp, x, wc, g, box, pix, out
+):
+    nc = tc.nc
+    with ExitStack() as ctx:
+        keep = ctx.enter_context(tc.tile_pool(name="keep", bufs=1))
+        work = ctx.enter_context(tc.tile_pool(name="work", bufs=3))
+        psum = ctx.enter_context(tc.psum_pool(name="psum", bufs=2))
+        ctx.enter_context(tc.manual_schedule())
+
+        fraw = [keep.tile([P, 2 * D], U8, name="fraw%d" % c, align_bytes=64) for c in range(CHUNKS)]
+        wp_raw = keep.tile([P, 4, K], BF16, align_bytes=64)
+        wc_raw = keep.tile([P, 4, K], BF16, align_bytes=64)
+        x_raw = keep.tile([P, B, D], BF16, align_bytes=64)
+        s4 = keep.tile([P, 1, 4], F32)
+        pixp = keep.tile([P, 16], BF16)
+        box_raw = keep.tile([P, B, 4], BF16)
+        g4 = keep.tile([P, 1, 4], BF16)
+
+        def load_f(c):
+            b, n0 = divmod(c * CH, N)
+            nc.sync.dma_start(
+                out=fraw[c][:].rearrange("p (j k) -> p j k", j=2),
+                in_=f_bytes[b, n0 : n0 + CH, :].rearrange("(r j) k -> r j k", j=2),
+            )
+
+        nc.scalar.dma_start(out=s4[:, 0, :], in_=f_scale.rearrange("a b (p t) -> p (a b t)", t=4))
+        nc.scalar.dma_start(out=pixp[:], in_=pix.rearrange("(p i) c -> p (i c)", i=8))
+        nc.scalar.dma_start(out=box_raw[:], in_=box.rearrange("b q c -> q b c"))
+        nc.scalar.dma_start(out=g4[:, 0, :], in_=g.rearrange("(p t) -> p t", t=4))
+        load_f(0)
+        nc.sync.dma_start(out=wp_raw[:], in_=wp.rearrange("(p j) w -> p j w", j=4))
+        load_f(1)
+        nc.sync.dma_start(out=x_raw[:], in_=x.rearrange("b q k -> q b k"))
+        nc.sync.dma_start(out=wc_raw[:], in_=wc.rearrange("(p j) w -> p j w", j=4))
+        for c in range(2, CHUNKS):
+            load_f(c)
+
+        warm = keep.tile([P, 1], F32)
+        nc.vector.memset(warm[:], 0.0)
+        nc.scalar.activation(out=warm[:], in_=warm[:], func=ACT.Sigmoid)
+        ident = keep.tile([P, P], F32)
+        make_identity(nc, ident[:])
+        identb = keep.tile([P, P], BF16)
+        nc.vector.tensor_copy(out=identb[:], in_=ident[:])
+        boxf = keep.tile([P, B, 4], F32)
+        box8 = keep.tile([P, B, 4], F32)
+        nc.gpsimd.tensor_copy(out=boxf[:], in_=box_raw[:])
+        nc.gpsimd.tensor_scalar(box8[:], box_raw[:], 8.0, 0.0, ALU.mult, ALU.add)
+        s8 = keep.tile([P, 1, 4, 2], F32)
+        nc.vector.tensor_copy(
+            out=s8[:].rearrange("p a (j u) e -> p (a j) (u e)", j=2),
+            in_=s4[:].to_broadcast([P, 2, 4]),
+        )
+
+        fb, tp, ft, fc, fs, pp, pt, pc, ps = {}, {}, {}, {}, {}, {}, {}, {}, {}
+
+        def W(c):
+            fwide = work.tile([P, 2 * D], BF16, name="fwide", align_bytes=64)
+            nc.vector.tensor_copy(out=fwide[:], in_=fraw[c][:].bitcast(FP8))
+            fb[c] = fwide
+
+        def T(c):
+            tbank = psum.tile([P, 512], F32, name="tbank")
+            words = fb[c][:].bitcast(F32)
+            for j in range(2):
+                for u in range(2):
+                    s = 2 * j + u
+                    nc.tensor.transpose(
+                        tbank[:, 128 * s : 128 * (s + 1)],
+                        words[:, 256 * j + u : 256 * (j + 1) : 2],
+                        ident[:],
+                    )
+            tp[c] = tbank
+
+        def E(c):
+            fgrp = work.tile([P, 1024], BF16, name="fgrp", align_bytes=64)
+            nc.vector.tensor_tensor(
+                out=fgrp[:].rearrange("p (r s e) -> p r s e", s=4, e=2),
+                in0=tp[c][:].bitcast(BF16).rearrange("p (s r e) -> p r s e", s=4, e=2),
+                in1=s8[:].to_broadcast([P, 128, 4, 2]),
+                op=ALU.mult,
+            )
+            ft[c] = fgrp
+
+        def quant(src, codes, scales):
+            nc.vector.quantize_mx(out=codes.bitcast(FP8X4), scales=scales, in_=src)
+
+        def Qf(c):
+            fcode = work.tile([P, CH], U32, name="fcode", align_bytes=64)
+            fscl = work.tile([P, CH], U8, name="fscl", align_bytes=64)
+            quant(ft[c][:], fcode[:], fscl[:])
+            fc[c], fs[c] = fcode, fscl
+
+        def mm(o, l, ls, r, rs):
+            nc.tensor.matmul_mx(
+                out=o, lhsT=l.bitcast(FP8X4), lhsT_scale=ls, rhs=r.bitcast(FP8X4), rhs_scale=rs,
+                start=True, stop=True,
+            )
+
+        def M(c):
+            pp[c] = []
+            for h in range(2):
+                pbank = psum.tile([P, 512], F32, name="pbank", bufs=4)
+                for t in range(4):
+                    ts = slice(128 * t, 128 * (t + 1))
+                    ns = slice(128 * h, 128 * (h + 1))
+                    mm(pbank[:, ts], wpc[:, ts], wps[:, ts], fc[c][:, ns], fs[c][:, ns])
+                pp[c].append(pbank)
+
+        def Pc(c):
+            pgrp = work.tile([P, 2, 512], BF16, name="pgrp", align_bytes=64)
+            for h in range(2):
+                nc.scalar.copy(
+                    out=pgrp[:, h, :].rearrange("p (n t) -> p n t", t=4),
+                    in_=pp[c][h][:].rearrange("p (t n) -> p n t", t=4),
+                )
+            pt[c] = pgrp
+
+        def R(c):
+            pcode = keep.tile([P, CH], U32, name="pcode%d" % c, align_bytes=64)
+            pscl = keep.tile([P, CH], U8, name="pscl%d" % c, align_bytes=64)
+            quant(pt[c][:].rearrange("p h w -> p (h w)"), pcode[:], pscl[:])
+            pc[c], ps[c] = pcode, pscl
+
+        mb, sm = {}, {}
+
+        def L(c):
+            k, h = divmod(c, 2)
+            b = c // (CHUNKS // B)
+            if h == 0:
+                mbank = psum.tile([P, 512], F32, name="mbank")
+                mb[k] = mbank
+            qs = slice(128 * b, 128 * (b + 1))
+            mm(mb[k][:, CH * h : CH * (h + 1)], cc[:, qs], cs[:, qs], pc[c][:], ps[c][:])
+
+        def SG(c, w):
+            h = c % 2
+            sig = work.tile([P, CH * w], F32, name="sig")
+            nc.scalar.activation(
+                out=sig[:], in_=mb[c // 2][:, CH * h : CH * (h + w)], func=ACT.Sigmoid, scale=3.0 / sqrt(K)
+            )
+            sm[c] = sig
+
+        def O(c, w):
+            b, n0 = divmod(c * CH, N)
+            res = work.tile([P, CH * w], F32, name="res")
+            ns = slice(n0, n0 + CH * w)
+            nc.vector.tensor_mul(res[:], sm[c][:], crop[b][0][:, ns])
+            nc.sync.dma_start(out=out[b, :, ns], in_=res[:])
+
+        pixb = []
+        for c in range(2):
+            for ih in range(2):
+                pixbank = psum.tile([P, 512], F32, name="pbank", bufs=4)
+                for i in range(4):
+                    m = 2 * (4 * ih + i) + c
+                    nc.tensor.matmul(
+                        pixbank[:, 128 * i : 128 * (i + 1)],
+                        lhsT=pixp[:, m : m + 1].to_broadcast([P, P]),
+                        rhs=identb[:],
+                        start=True,
+                        stop=True,
+                    )
+                pixb.append(pixbank)
+
+        crop = [[keep.tile([P, N], F32, name="crop%d%d" % (b, c)) for c in range(2)] for b in range(B)]
+
+        def absd(c, ih):
+            for b in range(B):
+                nc.scalar.activation(
+                    out=crop[b][c][:].rearrange("q (p i) -> q p i", i=8)[:, :, 4 * ih : 4 * ih + 4],
+                    in_=pixb[2 * c + ih][:].rearrange("q (i p) -> q p i", i=4),
+                    func=ACT.Abs,
+                    scale=-1.0,
+                    bias=boxf[:, b, c : c + 1],
+                )
+
+        def side(b, c):
+            nc.scalar.activation(
+                out=crop[b][c][:], in_=crop[b][c][:], func=ACT.Sigmoid, scale=-8.0,
+                bias=box8[:, b, 2 + c : 3 + c],
+            )
+
+        def both(b):
+            for h in range(2):
+                hs = slice(512 * h, 512 * (h + 1))
+                nc.gpsimd.tensor_mul(crop[b][0][:, hs], crop[b][0][:, hs], crop[b][1][:, hs])
+
+        wpc = keep.tile([P, K], U32, align_bytes=64)
+        wps = keep.tile([P, K], U8, align_bytes=64)
+        wcc = keep.tile([P, K], U32, align_bytes=64)
+        wcs = keep.tile([P, K], U8, align_bytes=64)
+        wpg = [keep.tile([P, 1024], BF16, name="wpg%d" % i, align_bytes=64) for i in range(2)]
+        wcg = keep.tile([P, 2048], BF16, align_bytes=64)
+
+        def wp_interleave(i):
+            nc.vector.tensor_copy(
+                out=wpg[i][:].rearrange("p (t m j) -> p t m j", t=2, j=4),
+                in_=wp_raw[:].rearrange("p j (m t) -> p t m j", t=4)[:, 2 * i : 2 * i + 2],
+            )
+
+        def wp_quant(i):
+            cs_ = slice(256 * i, 256 * (i + 1))
+            quant(wpg[i][:], wpc[:, cs_], wps[:, cs_])
+
+        def wc_interleave(t):
+            nc.gpsimd.tensor_scalar(
+                wcg[:].rearrange("p (t m j) -> p t m j", t=4, j=4)[:, t],
+                wc_raw[:].rearrange("p j (m t) -> p t m j", t=4)[:, t],
+                1.0, 0.0, ALU.mult, ALU.add,
+            )
+
+        xg = keep.tile([P, 1024], BF16, align_bytes=64)
+        xc = keep.tile([P, 256], U32, align_bytes=64)
+        xs = keep.tile([P, 256], U8, align_bytes=64)
+        th = keep.tile([P, 4, 256], F32)
+        cg = keep.tile([P, 2, 512], BF16, align_bytes=64)
+        cc = keep.tile([P, 256], U32, align_bytes=64)
+        cs = keep.tile([P, 256], U8, align_bytes=64)
+
+        def x_transpose():
+            xbank = psum.tile([P, 512], F32, name="tbank")
+            for b in range(B):
+                words = x_raw[:, b, :].bitcast(F32)
+                for u in range(2):
+                    s = 2 * b + u
+                    nc.tensor.transpose(xbank[:, 128 * s : 128 * (s + 1)], words[:, u::2], ident[:])
+            return xbank
+
+        def x_out(xbank):
+            nc.scalar.copy(
+                out=xg[:].bitcast(F32).rearrange("p (b q u) -> p b q u", b=2, u=2),
+                in_=xbank[:].rearrange("p (b u q) -> p b q u", b=2, u=2),
+            )
+
+        def h_matmul():
+            hb = []
+            for k in range(2):
+                hbank = psum.tile([P, 512], F32, name="mbank")
+                for i in range(2):
+                    ts = slice(128 * (2 * k + i), 128 * (2 * k + i + 1))
+                    mm(hbank[:, 256 * i : 256 * (i + 1)], wcc[:, ts], wcs[:, ts], xc[:], xs[:])
+                hb.append(hbank)
+            return hb
+
+        def h_tanh(hb, k):
+            nc.scalar.activation(
+                out=th[:, 2 * k : 2 * k + 2, :], in_=hb[k][:].rearrange("p (t q) -> p t q", t=2), func=ACT.Tanh
+            )
+
+        def c_gain(b):
+            nc.vector.tensor_tensor(
+                out=cg[:, b, :].rearrange("p (q t) -> p q t", t=4),
+                in0=th[:, :, 128 * b : 128 * (b + 1)].rearrange("p t q -> p q t"),
+                in1=g4[:].to_broadcast([P, 128, 4]),
+                op=ALU.mult,
+            )
+
+        W(0)
+        T(0)
+        W(1)
+        for t in range(4):
+            wc_interleave(t)
+        wp_interleave(0)
+        wp_interleave(1)
+        absd(0, 0)
+        absd(0, 1)
+        absd(1, 0)
+        absd(1, 1)
+        T(1)
+        E(0)
+        wp_quant(0)
+        wp_quant(1)
+        W(2)
+        Qf(0)
+        M(0)
+        xbank = x_transpose()
+        x_out(xbank)
+        side(0, 0)
+        hb = None
+        for i in range(CHUNKS + 1):
+            if i + 2 < CHUNKS:
+                T(i + 2)
+            if i + 1 < CHUNKS:
+                E(i + 1)
+            if i >= 1:
+                R(i - 1)
+            if i + 1 < CHUNKS:
+                Qf(i + 1)
+            if i == 0:
+                quant(xg[:], xc[:], xs[:])
+                quant(wcg[:, 0:1024], wcc[:, 0:256], wcs[:, 0:256])
+                quant(wcg[:, 1024:2048], wcc[:, 256:512], wcs[:, 256:512])
+            if i == 1:
+                c_gain(0)
+                c_gain(1)
+            if i == 2:
+                quant(cg[:].rearrange("p b w -> p (b w)"), cc[:], cs[:])
+            if i < CHUNKS:
+                Pc(i)
+            if i == 0:
+                hb = h_matmul()
+                h_tanh(hb, 0)
+                h_tanh(hb, 1)
+                side(0, 1)
+                both(0)
+            if i == 1:
+                side(1, 0)
+            if i == 2:
+                side(1, 1)
+                both(1)
+            if i == 2:
+                L(0)
+                L(1)
+            if i >= 3:
+                L(i - 1)
+            if i == 3:
+                SG(0, 2)
+            if i in (4, 6):
+                SG(i - 2, 2)
+            if i >= 7:
+                SG(i - 1, 1)
+            if i + 1 < CHUNKS:
+                M(i + 1)
+            if i + 3 < CHUNKS:
+                W(i + 3)
+            if i == 4:
+                O(0, 2)
+            if i in (5, 7):
+                O(i - 3, 2)
+            if i == 8:
+                O(6, 1)
+        O(7, 1)

@@ -19,6 +19,7 @@ ALU = mybir.AluOpType
 P = 128
 CH = 256
 CHUNKS = B * N // CH
+EARLY = (2, 3, 4, 5, 6, 7)
 
 
 def tile_prototypecoefficientsoftcropmasks_kernel(
@@ -47,40 +48,51 @@ def tile_prototypecoefficientsoftcropmasks_kernel(
                 in_=f_bytes[b, n0 : n0 + CH, :].rearrange("(r j) k -> r j k", j=2),
             )
 
-        nc.scalar.dma_start(out=s4[:, 0, :], in_=f_scale.rearrange("a b (p t) -> p (a b t)", t=4))
+        warm = keep.tile([P, 1], F32)
+        nc.vector.memset(warm[:], 0.0)
         nc.scalar.dma_start(out=pixp[:], in_=pix.rearrange("(p i) c -> p (i c)", i=8))
         nc.scalar.dma_start(out=box_raw[:], in_=box.rearrange("b q c -> q b c"))
+        nc.scalar.dma_start(out=s4[:, 0, :], in_=f_scale.rearrange("a b (p t) -> p (a b t)", t=4))
         nc.scalar.dma_start(out=g4[:, 0, :], in_=g.rearrange("(p t) -> p t", t=4))
+        nc.scalar.activation(out=warm[:], in_=warm[:], func=ACT.Sigmoid)
         load_f(0)
         nc.sync.dma_start(out=wp_raw[:], in_=wp.rearrange("(p j) w -> p j w", j=4))
         load_f(1)
         nc.sync.dma_start(out=x_raw[:], in_=x.rearrange("b q k -> q b k"))
+        sbc = keep.tile([P, D], F32)
+        nc.sync.dma_start(out=sbc[:], in_=f_scale.rearrange("a b k -> (a b k)").partition_broadcast(P))
+        load_f(2)
         nc.sync.dma_start(out=wc_raw[:], in_=wc.rearrange("(p j) w -> p j w", j=4))
-        for c in range(2, CHUNKS):
+        for c in range(3, CHUNKS):
             load_f(c)
 
-        warm = keep.tile([P, 1], F32)
-        nc.vector.memset(warm[:], 0.0)
-        nc.scalar.activation(out=warm[:], in_=warm[:], func=ACT.Sigmoid)
         ident = keep.tile([P, P], F32)
         make_identity(nc, ident[:])
         identb = keep.tile([P, P], BF16)
         nc.vector.tensor_copy(out=identb[:], in_=ident[:])
-        boxf = keep.tile([P, B, 4], F32)
         box8 = keep.tile([P, B, 4], F32)
-        nc.gpsimd.tensor_copy(out=boxf[:], in_=box_raw[:])
         nc.gpsimd.tensor_scalar(box8[:], box_raw[:], 8.0, 0.0, ALU.mult, ALU.add)
         s8 = keep.tile([P, 1, 4, 2], F32)
-        nc.vector.tensor_copy(
-            out=s8[:].rearrange("p a (j u) e -> p (a j) (u e)", j=2),
-            in_=s4[:].to_broadcast([P, 2, 4]),
-        )
+
+        def spread_scales():
+            nc.vector.tensor_copy(
+                out=s8[:].rearrange("p a (j u) e -> p (a j) (u e)", j=2),
+                in_=s4[:].to_broadcast([P, 2, 4]),
+            )
+
 
         fb, tp, ft, fc, fs, pp, pt, pc, ps = {}, {}, {}, {}, {}, {}, {}, {}, {}
 
         def W(c):
             fwide = work.tile([P, 2 * D], BF16, name="fwide", align_bytes=64)
-            nc.vector.tensor_copy(out=fwide[:], in_=fraw[c][:].bitcast(FP8))
+            if c in EARLY:
+                for j in range(2):
+                    ks = slice(D * j, D * (j + 1))
+                    nc.vector.tensor_tensor(
+                        out=fwide[:, ks], in0=fraw[c][:, ks].bitcast(FP8), in1=sbc[:], op=ALU.mult
+                    )
+            else:
+                nc.vector.tensor_copy(out=fwide[:], in_=fraw[c][:].bitcast(FP8))
             fb[c] = fwide
 
         def T(c):
@@ -98,13 +110,19 @@ def tile_prototypecoefficientsoftcropmasks_kernel(
 
         def E(c):
             fgrp = work.tile([P, 1024], BF16, name="fgrp", align_bytes=64)
+            ft[c] = fgrp
+            if c in EARLY:
+                nc.scalar.copy(
+                    out=fgrp[:].bitcast(F32).rearrange("p (r s) -> p r s", s=4),
+                    in_=tp[c][:].rearrange("p (s r) -> p r s", s=4),
+                )
+                return
             nc.vector.tensor_tensor(
                 out=fgrp[:].rearrange("p (r s e) -> p r s e", s=4, e=2),
                 in0=tp[c][:].bitcast(BF16).rearrange("p (s r e) -> p r s e", s=4, e=2),
                 in1=s8[:].to_broadcast([P, 128, 4, 2]),
                 op=ALU.mult,
             )
-            ft[c] = fgrp
 
         def quant(src, codes, scales):
             nc.vector.quantize_mx(out=codes.bitcast(FP8X4), scales=scales, in_=src)
@@ -134,7 +152,8 @@ def tile_prototypecoefficientsoftcropmasks_kernel(
         def Pc(c):
             pgrp = work.tile([P, 2, 512], BF16, name="pgrp", align_bytes=64)
             for h in range(2):
-                nc.scalar.copy(
+                copy = nc.vector.tensor_copy if c == CHUNKS - 1 and h == 1 else nc.scalar.copy
+                copy(
                     out=pgrp[:, h, :].rearrange("p (n t) -> p n t", t=4),
                     in_=pp[c][h][:].rearrange("p (t n) -> p n t", t=4),
                 )
@@ -172,20 +191,20 @@ def tile_prototypecoefficientsoftcropmasks_kernel(
             nc.vector.tensor_mul(res[:], sm[c][:], crop[b][0][:, ns])
             nc.sync.dma_start(out=out[b, :, ns], in_=res[:])
 
-        pixb = []
-        for c in range(2):
-            for ih in range(2):
-                pixbank = psum.tile([P, 512], F32, name="pbank", bufs=4)
-                for i in range(4):
-                    m = 2 * (4 * ih + i) + c
-                    nc.tensor.matmul(
-                        pixbank[:, 128 * i : 128 * (i + 1)],
-                        lhsT=pixp[:, m : m + 1].to_broadcast([P, P]),
-                        rhs=identb[:],
-                        start=True,
-                        stop=True,
-                    )
-                pixb.append(pixbank)
+        pixb = {}
+
+        def pix_spread(c, ih):
+            pixbank = psum.tile([P, 512], F32, name="pbank", bufs=4)
+            for i in range(4):
+                m = 2 * (4 * ih + i) + c
+                nc.tensor.matmul(
+                    pixbank[:, 128 * i : 128 * (i + 1)],
+                    lhsT=pixp[:, m : m + 1].to_broadcast([P, P]),
+                    rhs=identb[:],
+                    start=True,
+                    stop=True,
+                )
+            pixb[2 * c + ih] = pixbank
 
         crop = [[keep.tile([P, N], F32, name="crop%d%d" % (b, c)) for c in range(2)] for b in range(B)]
 
@@ -196,7 +215,7 @@ def tile_prototypecoefficientsoftcropmasks_kernel(
                     in_=pixb[2 * c + ih][:].rearrange("q (i p) -> q p i", i=4),
                     func=ACT.Abs,
                     scale=-1.0,
-                    bias=boxf[:, b, c : c + 1],
+                    bias=box_raw[:, b, c : c + 1],
                 )
 
         def side(b, c):
@@ -205,10 +224,9 @@ def tile_prototypecoefficientsoftcropmasks_kernel(
                 bias=box8[:, b, 2 + c : 3 + c],
             )
 
-        def both(b):
-            for h in range(2):
-                hs = slice(512 * h, 512 * (h + 1))
-                nc.gpsimd.tensor_mul(crop[b][0][:, hs], crop[b][0][:, hs], crop[b][1][:, hs])
+        def both(b, h):
+            hs = slice(512 * h, 512 * (h + 1))
+            nc.vector.tensor_mul(crop[b][0][:, hs], crop[b][0][:, hs], crop[b][1][:, hs])
 
         wpc = keep.tile([P, K], U32, align_bytes=64)
         wps = keep.tile([P, K], U8, align_bytes=64)
@@ -227,12 +245,15 @@ def tile_prototypecoefficientsoftcropmasks_kernel(
             cs_ = slice(256 * i, 256 * (i + 1))
             quant(wpg[i][:], wpc[:, cs_], wps[:, cs_])
 
-        def wc_interleave(t):
-            nc.gpsimd.tensor_scalar(
-                wcg[:].rearrange("p (t m j) -> p t m j", t=4, j=4)[:, t],
-                wc_raw[:].rearrange("p j (m t) -> p t m j", t=4)[:, t],
-                1.0, 0.0, ALU.mult, ALU.add,
+        def wc_interleave(i):
+            nc.vector.tensor_copy(
+                out=wcg[:].rearrange("p (t m j) -> p t m j", t=4, j=4)[:, 2 * i : 2 * i + 2],
+                in_=wc_raw[:].rearrange("p j (m t) -> p t m j", t=4)[:, 2 * i : 2 * i + 2],
             )
+
+        def wc_quant(i):
+            cs_ = slice(256 * i, 256 * (i + 1))
+            quant(wcg[:, 1024 * i : 1024 * (i + 1)], wcc[:, cs_], wcs[:, cs_])
 
         xg = keep.tile([P, 1024], BF16, align_bytes=64)
         xc = keep.tile([P, 256], U32, align_bytes=64)
@@ -281,77 +302,88 @@ def tile_prototypecoefficientsoftcropmasks_kernel(
             )
 
         W(0)
+        spread_scales()
+        pix_spread(0, 0)
         T(0)
-        W(1)
-        for t in range(4):
-            wc_interleave(t)
+        pix_spread(0, 1)
+        pix_spread(1, 0)
+        pix_spread(1, 1)
         wp_interleave(0)
         wp_interleave(1)
+        W(1)
+        T(1)
         absd(0, 0)
         absd(0, 1)
         absd(1, 0)
         absd(1, 1)
-        T(1)
+        side(0, 0)
         E(0)
         wp_quant(0)
         wp_quant(1)
-        W(2)
         Qf(0)
         M(0)
         xbank = x_transpose()
-        x_out(xbank)
-        side(0, 0)
         hb = None
         for i in range(CHUNKS + 1):
             if i + 2 < CHUNKS:
-                T(i + 2)
+                W(i + 2)
+            if i == 0:
+                x_out(xbank)
             if i + 1 < CHUNKS:
                 E(i + 1)
+            if i in (3, 4):
+                side(1, i - 3)
+            if i + 2 < CHUNKS:
+                T(i + 2)
+            if i == 0:
+                wc_interleave(0)
             if i >= 1:
                 R(i - 1)
+            if i == 1:
+                quant(xg[:], xc[:], xs[:])
             if i + 1 < CHUNKS:
                 Qf(i + 1)
             if i == 0:
-                quant(xg[:], xc[:], xs[:])
-                quant(wcg[:, 0:1024], wcc[:, 0:256], wcs[:, 0:256])
-                quant(wcg[:, 1024:2048], wcc[:, 256:512], wcs[:, 256:512])
+                wc_interleave(1)
             if i == 1:
+                wc_quant(0)
+                wc_quant(1)
+            if i == 3:
                 c_gain(0)
                 c_gain(1)
             if i == 2:
-                quant(cg[:].rearrange("p b w -> p (b w)"), cc[:], cs[:])
-            if i < CHUNKS:
-                Pc(i)
-            if i == 0:
-                hb = h_matmul()
                 h_tanh(hb, 0)
                 h_tanh(hb, 1)
-                side(0, 1)
-                both(0)
+            if i < CHUNKS:
+                Pc(i)
             if i == 1:
-                side(1, 0)
-            if i == 2:
-                side(1, 1)
-                both(1)
-            if i == 2:
-                L(0)
-                L(1)
-            if i >= 3:
-                L(i - 1)
-            if i == 3:
-                SG(0, 2)
-            if i in (4, 6):
-                SG(i - 2, 2)
-            if i >= 7:
-                SG(i - 1, 1)
+                side(0, 1)
             if i + 1 < CHUNKS:
                 M(i + 1)
-            if i + 3 < CHUNKS:
-                W(i + 3)
+            if i == 1:
+                hb = h_matmul()
             if i == 4:
+                quant(cg[:].rearrange("p b w -> p (b w)"), cc[:], cs[:])
+                for c in range(4):
+                    L(c)
+            if i >= 5:
+                L(i - 1)
+            if i == 4:
+                both(0, 0)
+                both(0, 1)
+                SG(0, 2)
+            if i == 5:
                 O(0, 2)
-            if i in (5, 7):
-                O(i - 3, 2)
+                SG(2, 2)
+                both(1, 0)
+            if i == 6:
+                O(2, 2)
+                SG(4, 2)
+                both(1, 1)
+            if i == 7:
+                O(4, 2)
+                SG(6, 1)
             if i == 8:
                 O(6, 1)
+                SG(7, 1)
         O(7, 1)

@@ -17,9 +17,14 @@ ACT = mybir.ActivationFunctionType
 ALU = mybir.AluOpType
 
 P = 128
-CH = 256
-CHUNKS = B * N // CH
-EARLY = (2, 3, 4, 5, 6, 7)
+CHUNK = 256
+CHUNKS = B * N // CHUNK
+PER_BATCH = N // CHUNK
+BANK = 512
+
+SCALED_AT_ONCE_FROM = 3
+
+WARM_UP = 2
 
 
 def tile_prototypecoefficientsoftcropmasks_kernel(
@@ -32,358 +37,393 @@ def tile_prototypecoefficientsoftcropmasks_kernel(
         psum = ctx.enter_context(tc.psum_pool(name="psum", bufs=2))
         ctx.enter_context(tc.manual_schedule())
 
-        fraw = [keep.tile([P, 2 * D], U8, name="fraw%d" % c, align_bytes=64) for c in range(CHUNKS)]
+        f_raw = [keep.tile([P, 2 * D], U8, name="f_raw%d" % c, align_bytes=64) for c in range(CHUNKS)]
         wp_raw = keep.tile([P, 4, K], BF16, align_bytes=64)
         wc_raw = keep.tile([P, 4, K], BF16, align_bytes=64)
         x_raw = keep.tile([P, B, D], BF16, align_bytes=64)
-        s4 = keep.tile([P, 1, 4], F32)
-        pixp = keep.tile([P, 16], BF16)
+        scale_kt = keep.tile([P, 1, 4], F32)
+        scale_row = keep.tile([P, D], F32)
+        gain_kt = keep.tile([P, 1, 4], BF16)
         box_raw = keep.tile([P, B, 4], BF16)
-        g4 = keep.tile([P, 1, 4], BF16)
+        pix_rows = keep.tile([P, 512], BF16)
+        nc.vector.memset(pix_rows[:], 0.0)
 
         def load_f(c):
-            b, n0 = divmod(c * CH, N)
+            b, n0 = divmod(c * CHUNK, N)
             nc.sync.dma_start(
-                out=fraw[c][:].rearrange("p (j k) -> p j k", j=2),
-                in_=f_bytes[b, n0 : n0 + CH, :].rearrange("(r j) k -> r j k", j=2),
+                out=f_raw[c][:].rearrange("p (j k) -> p j k", j=2),
+                in_=f_bytes[b, n0 : n0 + CHUNK, :].rearrange("(r j) k -> r j k", j=2),
             )
 
-        warm = keep.tile([P, 1], F32)
-        nc.vector.memset(warm[:], 0.0)
-        nc.scalar.dma_start(out=pixp[:], in_=pix.rearrange("(p i) c -> p (i c)", i=8))
+        table = keep.tile([P, 1], F32)
+        nc.vector.memset(table[:], 0.0)
+        nc.scalar.dma_start(out=scale_kt[:, 0, :], in_=f_scale.rearrange("a b (p t) -> p (a b t)", t=4))
+        nc.scalar.dma_start(out=pix_rows[0:4, :], in_=pix.rearrange("(r n) c -> r (n c)", r=4))
         nc.scalar.dma_start(out=box_raw[:], in_=box.rearrange("b q c -> q b c"))
-        nc.scalar.dma_start(out=s4[:, 0, :], in_=f_scale.rearrange("a b (p t) -> p (a b t)", t=4))
-        nc.scalar.dma_start(out=g4[:, 0, :], in_=g.rearrange("(p t) -> p t", t=4))
-        nc.scalar.activation(out=warm[:], in_=warm[:], func=ACT.Sigmoid)
+        nc.scalar.dma_start(out=gain_kt[:, 0, :], in_=g.rearrange("(p t) -> p t", t=4))
+        nc.scalar.activation(out=table[:], in_=table[:], func=ACT.Sigmoid)
         load_f(0)
         nc.sync.dma_start(out=wp_raw[:], in_=wp.rearrange("(p j) w -> p j w", j=4))
         load_f(1)
         nc.sync.dma_start(out=x_raw[:], in_=x.rearrange("b q k -> q b k"))
-        sbc = keep.tile([P, D], F32)
-        nc.sync.dma_start(out=sbc[:], in_=f_scale.rearrange("a b k -> (a b k)").partition_broadcast(P))
         load_f(2)
         nc.sync.dma_start(out=wc_raw[:], in_=wc.rearrange("(p j) w -> p j w", j=4))
         for c in range(3, CHUNKS):
             load_f(c)
+        nc.sync.dma_start(out=scale_row[:], in_=f_scale.rearrange("a b k -> (a b k)").partition_broadcast(P))
 
+        zero = keep.tile([P, BANK], BF16)
+        nc.vector.memset(zero[:], 0.0)
+        warm_bank = psum.tile([P, BANK], F32, name="m_bank")
+        for k in range(WARM_UP):
+            nc.tensor.matmul(warm_bank[:], lhsT=zero[:, 0:P], rhs=zero[:], start=True, stop=True)
         ident = keep.tile([P, P], F32)
         make_identity(nc, ident[:])
-        identb = keep.tile([P, P], BF16)
-        nc.vector.tensor_copy(out=identb[:], in_=ident[:])
+        ident_bf = keep.tile([P, P], BF16)
+        nc.vector.tensor_copy(out=ident_bf[:], in_=ident[:])
         box8 = keep.tile([P, B, 4], F32)
         nc.gpsimd.tensor_scalar(box8[:], box_raw[:], 8.0, 0.0, ALU.mult, ALU.add)
-        s8 = keep.tile([P, 1, 4, 2], F32)
+        scale_jue = keep.tile([P, 1, 4, 2], F32)
+        nc.vector.tensor_copy(
+            out=scale_jue[:].rearrange("p a (j u) e -> p (a j) (u e)", j=2),
+            in_=scale_kt[:].to_broadcast([P, 2, 4]),
+        )
 
-        def spread_scales():
-            nc.vector.tensor_copy(
-                out=s8[:].rearrange("p a (j u) e -> p (a j) (u e)", j=2),
-                in_=s4[:].to_broadcast([P, 2, 4]),
+        def quantise(values, codes, scales):
+            nc.vector.quantize_mx(out=codes.bitcast(FP8X4), scales=scales, in_=values)
+
+        def multiply(acc, left, left_scales, right, right_scales):
+            nc.tensor.matmul_mx(
+                out=acc,
+                lhsT=left.bitcast(FP8X4),
+                lhsT_scale=left_scales,
+                rhs=right.bitcast(FP8X4),
+                rhs_scale=right_scales,
+                start=True,
+                stop=True,
             )
 
+        wp_grouped = keep.tile([P, 4 * K], BF16, align_bytes=64)
+        wp_codes = keep.tile([P, K], U32, align_bytes=64)
+        wp_scales = keep.tile([P, K], U8, align_bytes=64)
+        wc_grouped = keep.tile([P, 4 * K], BF16, align_bytes=64)
+        wc_codes = keep.tile([P, K], U32, align_bytes=64)
+        wc_scales = keep.tile([P, K], U8, align_bytes=64)
 
-        fb, tp, ft, fc, fs, pp, pt, pc, ps = {}, {}, {}, {}, {}, {}, {}, {}, {}
+        def group_wp(half):
+            ts = slice(2 * half, 2 * half + 2)
+            nc.vector.tensor_copy(
+                out=wp_grouped[:].rearrange("p (t m j) -> p t m j", t=4, j=4)[:, ts],
+                in_=wp_raw[:].rearrange("p j (m t) -> p t m j", t=4)[:, ts],
+            )
 
-        def W(c):
-            fwide = work.tile([P, 2 * D], BF16, name="fwide", align_bytes=64)
-            if c in EARLY:
+        def group_wc(half):
+            for t in (2 * half, 2 * half + 1):
+                nc.gpsimd.tensor_scalar(
+                    wc_grouped[:].rearrange("p (t m j) -> p t m j", t=4, j=4)[:, t],
+                    wc_raw[:].rearrange("p j (m t) -> p t m j", t=4)[:, t],
+                    1.0,
+                    0.0,
+                    ALU.mult,
+                    ALU.add,
+                )
+
+        wide, turned, f_grouped, f_codes, f_scales = {}, {}, {}, {}, {}
+        p_banks, p_grouped, p_codes, p_scales = {}, {}, {}, {}
+        m_banks, sigmoids = {}, {}
+
+        def widen(c):
+            f_wide = work.tile([P, 2 * D], BF16, bufs=4, align_bytes=64)
+            if c < SCALED_AT_ONCE_FROM:
+                nc.vector.tensor_copy(out=f_wide[:], in_=f_raw[c][:].bitcast(FP8))
+            else:
                 for j in range(2):
                     ks = slice(D * j, D * (j + 1))
                     nc.vector.tensor_tensor(
-                        out=fwide[:, ks], in0=fraw[c][:, ks].bitcast(FP8), in1=sbc[:], op=ALU.mult
+                        out=f_wide[:, ks], in0=f_raw[c][:, ks].bitcast(FP8), in1=scale_row[:], op=ALU.mult
                     )
-            else:
-                nc.vector.tensor_copy(out=fwide[:], in_=fraw[c][:].bitcast(FP8))
-            fb[c] = fwide
+            wide[c] = f_wide
 
-        def T(c):
-            tbank = psum.tile([P, 512], F32, name="tbank")
-            words = fb[c][:].bitcast(F32)
+        def turn(c):
+            turn_bank = psum.tile([P, BANK], F32, name="turn_bank")
+            words = wide[c][:].bitcast(F32)
             for j in range(2):
                 for u in range(2):
                     s = 2 * j + u
                     nc.tensor.transpose(
-                        tbank[:, 128 * s : 128 * (s + 1)],
-                        words[:, 256 * j + u : 256 * (j + 1) : 2],
-                        ident[:],
+                        turn_bank[:, P * s : P * (s + 1)], words[:, 256 * j + u : 256 * (j + 1) : 2], ident[:]
                     )
-            tp[c] = tbank
+            turned[c] = turn_bank
 
-        def E(c):
-            fgrp = work.tile([P, 1024], BF16, name="fgrp", align_bytes=64)
-            ft[c] = fgrp
-            if c in EARLY:
+        def group_f(c):
+            f_group = work.tile([P, 4 * CHUNK], BF16, align_bytes=64)
+            if c < SCALED_AT_ONCE_FROM:
+                nc.vector.tensor_tensor(
+                    out=f_group[:].rearrange("p (r s e) -> p r s e", s=4, e=2),
+                    in0=turned[c][:].bitcast(BF16).rearrange("p (s r e) -> p r s e", s=4, e=2),
+                    in1=scale_jue[:].to_broadcast([P, P, 4, 2]),
+                    op=ALU.mult,
+                )
+            else:
                 nc.scalar.copy(
-                    out=fgrp[:].bitcast(F32).rearrange("p (r s) -> p r s", s=4),
-                    in_=tp[c][:].rearrange("p (s r) -> p r s", s=4),
+                    out=f_group[:].bitcast(F32).rearrange("p (r s) -> p r s", s=4),
+                    in_=turned[c][:].rearrange("p (s r) -> p r s", s=4),
                 )
-                return
-            nc.vector.tensor_tensor(
-                out=fgrp[:].rearrange("p (r s e) -> p r s e", s=4, e=2),
-                in0=tp[c][:].bitcast(BF16).rearrange("p (s r e) -> p r s e", s=4, e=2),
-                in1=s8[:].to_broadcast([P, 128, 4, 2]),
-                op=ALU.mult,
-            )
+            f_grouped[c] = f_group
 
-        def quant(src, codes, scales):
-            nc.vector.quantize_mx(out=codes.bitcast(FP8X4), scales=scales, in_=src)
+        def quantise_f(c):
+            f_code = work.tile([P, CHUNK], U32, align_bytes=64)
+            f_scl = work.tile([P, CHUNK], U8, align_bytes=64)
+            quantise(f_grouped[c][:], f_code[:], f_scl[:])
+            f_codes[c], f_scales[c] = f_code, f_scl
 
-        def Qf(c):
-            fcode = work.tile([P, CH], U32, name="fcode", align_bytes=64)
-            fscl = work.tile([P, CH], U8, name="fscl", align_bytes=64)
-            quant(ft[c][:], fcode[:], fscl[:])
-            fc[c], fs[c] = fcode, fscl
-
-        def mm(o, l, ls, r, rs):
-            nc.tensor.matmul_mx(
-                out=o, lhsT=l.bitcast(FP8X4), lhsT_scale=ls, rhs=r.bitcast(FP8X4), rhs_scale=rs,
-                start=True, stop=True,
-            )
-
-        def M(c):
-            pp[c] = []
+        def take_p_banks(c):
+            p_banks[c] = []
             for h in range(2):
-                pbank = psum.tile([P, 512], F32, name="pbank", bufs=4)
+                p_bank = psum.tile([P, BANK], F32, name="p_bank", bufs=4)
+                p_banks[c].append(p_bank)
+
+        def spare(c):
+            multiply(p_banks[c][0][:], wp_codes[:, 0:P], wp_scales[:, 0:P], wp_codes[:], wp_scales[:])
+
+        def project(c):
+            for h in range(2):
                 for t in range(4):
-                    ts = slice(128 * t, 128 * (t + 1))
-                    ns = slice(128 * h, 128 * (h + 1))
-                    mm(pbank[:, ts], wpc[:, ts], wps[:, ts], fc[c][:, ns], fs[c][:, ns])
-                pp[c].append(pbank)
+                    ts = slice(P * t, P * (t + 1))
+                    ns = slice(P * h, P * (h + 1))
+                    multiply(
+                        p_banks[c][h][:, ts], wp_codes[:, ts], wp_scales[:, ts], f_codes[c][:, ns], f_scales[c][:, ns]
+                    )
 
-        def Pc(c):
-            pgrp = work.tile([P, 2, 512], BF16, name="pgrp", align_bytes=64)
+        def group_p(c):
+            p_group = work.tile([P, 2, BANK], BF16, align_bytes=64)
             for h in range(2):
-                copy = nc.vector.tensor_copy if c == CHUNKS - 1 and h == 1 else nc.scalar.copy
+                copy = nc.vector.tensor_copy if (c, h) == (CHUNKS - 1, 1) else nc.scalar.copy
                 copy(
-                    out=pgrp[:, h, :].rearrange("p (n t) -> p n t", t=4),
-                    in_=pp[c][h][:].rearrange("p (t n) -> p n t", t=4),
+                    out=p_group[:, h, :].rearrange("p (n t) -> p n t", t=4),
+                    in_=p_banks[c][h][:].rearrange("p (t n) -> p n t", t=4),
                 )
-            pt[c] = pgrp
+            p_grouped[c] = p_group
 
-        def R(c):
-            pcode = keep.tile([P, CH], U32, name="pcode%d" % c, align_bytes=64)
-            pscl = keep.tile([P, CH], U8, name="pscl%d" % c, align_bytes=64)
-            quant(pt[c][:].rearrange("p h w -> p (h w)"), pcode[:], pscl[:])
-            pc[c], ps[c] = pcode, pscl
+        def quantise_p(c):
+            p_code = keep.tile([P, CHUNK], U32, name="p_code%d" % c, align_bytes=64)
+            p_scl = keep.tile([P, CHUNK], U8, name="p_scl%d" % c, align_bytes=64)
+            quantise(p_grouped[c][:].rearrange("p h w -> p (h w)"), p_code[:], p_scl[:])
+            p_codes[c], p_scales[c] = p_code, p_scl
 
-        mb, sm = {}, {}
-
-        def L(c):
-            k, h = divmod(c, 2)
-            b = c // (CHUNKS // B)
-            if h == 0:
-                mbank = psum.tile([P, 512], F32, name="mbank")
-                mb[k] = mbank
-            qs = slice(128 * b, 128 * (b + 1))
-            mm(mb[k][:, CH * h : CH * (h + 1)], cc[:, qs], cs[:, qs], pc[c][:], ps[c][:])
-
-        def SG(c, w):
-            h = c % 2
-            sig = work.tile([P, CH * w], F32, name="sig")
-            nc.scalar.activation(
-                out=sig[:], in_=mb[c // 2][:, CH * h : CH * (h + w)], func=ACT.Sigmoid, scale=3.0 / sqrt(K)
+        def logits(c):
+            pair, half = divmod(c, 2)
+            if half == 0:
+                m_bank = psum.tile([P, BANK], F32, name="m_bank")
+                m_banks[pair] = m_bank
+            qs = slice(Q * (c // PER_BATCH), Q * (c // PER_BATCH + 1))
+            multiply(
+                m_banks[pair][:, CHUNK * half : CHUNK * (half + 1)],
+                c_codes[:, qs],
+                c_scales[:, qs],
+                p_codes[c][:],
+                p_scales[c][:],
             )
-            sm[c] = sig
 
-        def O(c, w):
-            b, n0 = divmod(c * CH, N)
-            res = work.tile([P, CH * w], F32, name="res")
-            ns = slice(n0, n0 + CH * w)
-            nc.vector.tensor_mul(res[:], sm[c][:], crop[b][0][:, ns])
-            nc.sync.dma_start(out=out[b, :, ns], in_=res[:])
+        def squash(c, count):
+            half = c % 2
+            sigmoid_m = work.tile([P, CHUNK * count], F32, bufs=7)
+            nc.scalar.activation(
+                out=sigmoid_m[:],
+                in_=m_banks[c // 2][:, CHUNK * half : CHUNK * (half + count)],
+                func=ACT.Sigmoid,
+                scale=3.0 / sqrt(K),
+            )
+            sigmoids[c] = sigmoid_m
 
-        pixb = {}
+        def mask(c, count):
+            b, n0 = divmod(c * CHUNK, N)
+            ns = slice(n0, n0 + CHUNK * count)
+            result = work.tile([P, CHUNK * count], F32, bufs=7)
+            nc.vector.tensor_mul(result[:], sigmoids[c][:], sides[b][0][:, ns])
+            nc.sync.dma_start(out=out[b, :, ns], in_=result[:])
 
-        def pix_spread(c, ih):
-            pixbank = psum.tile([P, 512], F32, name="pbank", bufs=4)
-            for i in range(4):
-                m = 2 * (4 * ih + i) + c
+        sides = [[keep.tile([P, N], F32, name="side%d%d" % (b, a)) for a in range(2)] for b in range(B)]
+        pix_banks = {}
+
+        def spread_pixels(axis, half):
+            pix_bank = psum.tile([P, BANK], F32, name="p_bank", bufs=4)
+            for i in range(2):
+                r = 2 * half + i
                 nc.tensor.matmul(
-                    pixbank[:, 128 * i : 128 * (i + 1)],
-                    lhsT=pixp[:, m : m + 1].to_broadcast([P, P]),
-                    rhs=identb[:],
+                    pix_bank[:, 256 * i : 256 * (i + 1)],
+                    lhsT=ident_bf[:, r : r + 1].to_broadcast([P, P]),
+                    rhs=pix_rows[:, axis::2],
                     start=True,
                     stop=True,
                 )
-            pixb[2 * c + ih] = pixbank
+            pix_banks[axis, half] = pix_bank
 
-        crop = [[keep.tile([P, N], F32, name="crop%d%d" % (b, c)) for c in range(2)] for b in range(B)]
-
-        def absd(c, ih):
+        def distance(axis, half):
             for b in range(B):
                 nc.scalar.activation(
-                    out=crop[b][c][:].rearrange("q (p i) -> q p i", i=8)[:, :, 4 * ih : 4 * ih + 4],
-                    in_=pixb[2 * c + ih][:].rearrange("q (i p) -> q p i", i=4),
+                    out=sides[b][axis][:, BANK * half : BANK * (half + 1)],
+                    in_=pix_banks[axis, half][:],
                     func=ACT.Abs,
                     scale=-1.0,
-                    bias=box_raw[:, b, c : c + 1],
+                    bias=box_raw[:, b, axis : axis + 1],
                 )
 
-        def side(b, c):
+        def side(b, axis):
             nc.scalar.activation(
-                out=crop[b][c][:], in_=crop[b][c][:], func=ACT.Sigmoid, scale=-8.0,
-                bias=box8[:, b, 2 + c : 3 + c],
+                out=sides[b][axis][:],
+                in_=sides[b][axis][:],
+                func=ACT.Sigmoid,
+                scale=-8.0,
+                bias=box8[:, b, 2 + axis : 3 + axis],
             )
 
-        def both(b, h):
-            hs = slice(512 * h, 512 * (h + 1))
-            nc.vector.tensor_mul(crop[b][0][:, hs], crop[b][0][:, hs], crop[b][1][:, hs])
+        def crop(b, half):
+            ns = slice(BANK * half, BANK * (half + 1))
+            nc.vector.tensor_mul(sides[b][0][:, ns], sides[b][0][:, ns], sides[b][1][:, ns])
 
-        wpc = keep.tile([P, K], U32, align_bytes=64)
-        wps = keep.tile([P, K], U8, align_bytes=64)
-        wcc = keep.tile([P, K], U32, align_bytes=64)
-        wcs = keep.tile([P, K], U8, align_bytes=64)
-        wpg = [keep.tile([P, 1024], BF16, name="wpg%d" % i, align_bytes=64) for i in range(2)]
-        wcg = keep.tile([P, 2048], BF16, align_bytes=64)
+        x_grouped = keep.tile([P, 4 * B * Q], BF16, align_bytes=64)
+        x_codes = keep.tile([P, B * Q], U32, align_bytes=64)
+        x_scales = keep.tile([P, B * Q], U8, align_bytes=64)
+        tanh_h = keep.tile([P, 4, B * Q], F32)
+        c_grouped = keep.tile([P, B, 4 * Q], BF16, align_bytes=64)
+        c_codes = keep.tile([P, B * Q], U32, align_bytes=64)
+        c_scales = keep.tile([P, B * Q], U8, align_bytes=64)
 
-        def wp_interleave(i):
-            nc.vector.tensor_copy(
-                out=wpg[i][:].rearrange("p (t m j) -> p t m j", t=2, j=4),
-                in_=wp_raw[:].rearrange("p j (m t) -> p t m j", t=4)[:, 2 * i : 2 * i + 2],
-            )
-
-        def wp_quant(i):
-            cs_ = slice(256 * i, 256 * (i + 1))
-            quant(wpg[i][:], wpc[:, cs_], wps[:, cs_])
-
-        def wc_interleave(i):
-            nc.vector.tensor_copy(
-                out=wcg[:].rearrange("p (t m j) -> p t m j", t=4, j=4)[:, 2 * i : 2 * i + 2],
-                in_=wc_raw[:].rearrange("p j (m t) -> p t m j", t=4)[:, 2 * i : 2 * i + 2],
-            )
-
-        def wc_quant(i):
-            cs_ = slice(256 * i, 256 * (i + 1))
-            quant(wcg[:, 1024 * i : 1024 * (i + 1)], wcc[:, cs_], wcs[:, cs_])
-
-        xg = keep.tile([P, 1024], BF16, align_bytes=64)
-        xc = keep.tile([P, 256], U32, align_bytes=64)
-        xs = keep.tile([P, 256], U8, align_bytes=64)
-        th = keep.tile([P, 4, 256], F32)
-        cg = keep.tile([P, 2, 512], BF16, align_bytes=64)
-        cc = keep.tile([P, 256], U32, align_bytes=64)
-        cs = keep.tile([P, 256], U8, align_bytes=64)
-
-        def x_transpose():
-            xbank = psum.tile([P, 512], F32, name="tbank")
+        def turn_x():
+            x_bank = psum.tile([P, BANK], F32, name="turn_bank")
             for b in range(B):
                 words = x_raw[:, b, :].bitcast(F32)
                 for u in range(2):
                     s = 2 * b + u
-                    nc.tensor.transpose(xbank[:, 128 * s : 128 * (s + 1)], words[:, u::2], ident[:])
-            return xbank
+                    nc.tensor.transpose(x_bank[:, P * s : P * (s + 1)], words[:, u::2], ident[:])
+            return x_bank
 
-        def x_out(xbank):
+        def group_x(x_bank):
             nc.scalar.copy(
-                out=xg[:].bitcast(F32).rearrange("p (b q u) -> p b q u", b=2, u=2),
-                in_=xbank[:].rearrange("p (b u q) -> p b q u", b=2, u=2),
+                out=x_grouped[:].bitcast(F32).rearrange("p (b q u) -> p b q u", b=B, u=2),
+                in_=x_bank[:].rearrange("p (b u q) -> p b q u", b=B, u=2),
             )
 
-        def h_matmul():
-            hb = []
+        def hidden():
+            h_banks = []
             for k in range(2):
-                hbank = psum.tile([P, 512], F32, name="mbank")
+                h_bank = psum.tile([P, BANK], F32, name="m_bank")
                 for i in range(2):
-                    ts = slice(128 * (2 * k + i), 128 * (2 * k + i + 1))
-                    mm(hbank[:, 256 * i : 256 * (i + 1)], wcc[:, ts], wcs[:, ts], xc[:], xs[:])
-                hb.append(hbank)
-            return hb
+                    ts = slice(P * (2 * k + i), P * (2 * k + i + 1))
+                    multiply(h_bank[:, 256 * i : 256 * (i + 1)], wc_codes[:, ts], wc_scales[:, ts], x_codes[:], x_scales[:])
+                h_banks.append(h_bank)
+            return h_banks
 
-        def h_tanh(hb, k):
-            nc.scalar.activation(
-                out=th[:, 2 * k : 2 * k + 2, :], in_=hb[k][:].rearrange("p (t q) -> p t q", t=2), func=ACT.Tanh
-            )
+        def squash_h(h_banks):
+            for k in range(2):
+                nc.scalar.activation(
+                    out=tanh_h[:, 2 * k : 2 * k + 2, :],
+                    in_=h_banks[k][:].rearrange("p (t q) -> p t q", t=2),
+                    func=ACT.Tanh,
+                )
 
-        def c_gain(b):
+        def gain(b):
             nc.vector.tensor_tensor(
-                out=cg[:, b, :].rearrange("p (q t) -> p q t", t=4),
-                in0=th[:, :, 128 * b : 128 * (b + 1)].rearrange("p t q -> p q t"),
-                in1=g4[:].to_broadcast([P, 128, 4]),
+                out=c_grouped[:, b, :].rearrange("p (q t) -> p q t", t=4),
+                in0=tanh_h[:, :, Q * b : Q * (b + 1)].rearrange("p t q -> p q t"),
+                in1=gain_kt[:].to_broadcast([P, Q, 4]),
                 op=ALU.mult,
             )
 
-        W(0)
-        spread_scales()
-        pix_spread(0, 0)
-        T(0)
-        pix_spread(0, 1)
-        pix_spread(1, 0)
-        pix_spread(1, 1)
-        wp_interleave(0)
-        wp_interleave(1)
-        W(1)
-        T(1)
-        absd(0, 0)
-        absd(0, 1)
-        absd(1, 0)
-        absd(1, 1)
+        widen(0)
+        group_wp(0)
+        widen(1)
+        group_wp(1)
+        spread_pixels(0, 0)
+        spread_pixels(0, 1)
+        spread_pixels(1, 0)
+        turn(0)
+        spread_pixels(1, 1)
+        turn(1)
+        x_bank = turn_x()
+        for axis in range(2):
+            for half in range(2):
+                distance(axis, half)
         side(0, 0)
-        E(0)
-        wp_quant(0)
-        wp_quant(1)
-        Qf(0)
-        M(0)
-        xbank = x_transpose()
-        hb = None
+        group_f(0)
+        quantise_f(0)
+        quantise(wp_grouped[:], wp_codes[:], wp_scales[:])
+        take_p_banks(0)
+        project(0)
+
         for i in range(CHUNKS + 1):
             if i + 2 < CHUNKS:
-                W(i + 2)
-            if i == 0:
-                x_out(xbank)
-            if i + 1 < CHUNKS:
-                E(i + 1)
-            if i in (3, 4):
-                side(1, i - 3)
-            if i + 2 < CHUNKS:
-                T(i + 2)
-            if i == 0:
-                wc_interleave(0)
-            if i >= 1:
-                R(i - 1)
+                widen(i + 2)
+
+            if i < 2:
+                group_wc(i)
             if i == 1:
-                quant(xg[:], xc[:], xs[:])
-            if i + 1 < CHUNKS:
-                Qf(i + 1)
-            if i == 0:
-                wc_interleave(1)
-            if i == 1:
-                wc_quant(0)
-                wc_quant(1)
-            if i == 3:
-                c_gain(0)
-                c_gain(1)
+                group_x(x_bank)
             if i == 2:
-                h_tanh(hb, 0)
-                h_tanh(hb, 1)
-            if i < CHUNKS:
-                Pc(i)
-            if i == 1:
-                side(0, 1)
-            if i + 1 < CHUNKS:
-                M(i + 1)
-            if i == 1:
-                hb = h_matmul()
+                side(1, 0)
+                crop(0, 0)
+                h_banks = hidden()
+            if i == 3:
+                squash_h(h_banks)
             if i == 4:
-                quant(cg[:].rearrange("p b w -> p (b w)"), cc[:], cs[:])
-                for c in range(4):
-                    L(c)
-            if i >= 5:
-                L(i - 1)
-            if i == 4:
-                both(0, 0)
-                both(0, 1)
-                SG(0, 2)
+                logits(0)
+                logits(1)
+                logits(2)
             if i == 5:
-                O(0, 2)
-                SG(2, 2)
-                both(1, 0)
-            if i == 6:
-                O(2, 2)
-                SG(4, 2)
-                both(1, 1)
+                squash(0, 2)
             if i == 7:
-                O(4, 2)
-                SG(6, 1)
+                crop(1, 1)
+                logits(4)
+                logits(5)
             if i == 8:
-                O(6, 1)
-                SG(7, 1)
-        O(7, 1)
+                squash(6, 1)
+
+            if i + 1 < CHUNKS:
+                group_f(i + 1)
+            if i + 2 < CHUNKS:
+                turn(i + 2)
+            if i + 1 < CHUNKS:
+                take_p_banks(i + 1)
+                spare(i + 1)
+
+            if i == 0:
+                side(0, 1)
+            if i == 6:
+                squash(2, 2)
+            if i >= 1:
+                quantise_p(i - 1)
+            if i == 3:
+                gain(0)
+            if i + 1 < CHUNKS:
+                quantise_f(i + 1)
+            if i == 1:
+                quantise(wc_grouped[:], wc_codes[:], wc_scales[:])
+                quantise(x_grouped[:], x_codes[:], x_scales[:])
+            if i == 3:
+                gain(1)
+                crop(0, 1)
+                quantise(c_grouped[:].rearrange("p b w -> p (b w)"), c_codes[:], c_scales[:])
+            if i == 5:
+                mask(0, 2)
+                crop(1, 0)
+            if i == 6:
+                mask(2, 2)
+
+            if i < CHUNKS:
+                group_p(i)
+            if i == 4:
+                side(1, 1)
+            if i == 5:
+                logits(3)
+            if i == 7:
+                squash(4, 2)
+                logits(6)
+            if i + 1 < CHUNKS:
+                project(i + 1)
+
+        logits(7)
+        squash(7, 1)
+        mask(4, 2)
+        mask(6, 1)
+        mask(7, 1)

from contextlib import ExitStack
from math import sqrt

import concourse.mybir as mybir
from concourse.masks import make_identity

B, Q, N, D, K = 2, 128, 1024, 512, 512
FLOPS = 2 * B * N * D * K + 2 * B * Q * D * K + 2 * B * Q * N * K

F32 = mybir.dt.float32
BF16 = mybir.dt.bfloat16
U32 = mybir.dt.uint32
U8 = mybir.dt.uint8
FP8 = mybir.dt.float8_e4m3fn
FP8X4 = mybir.dt.float8_e4m3fn_x4
ACT = mybir.ActivationFunctionType
ALU = mybir.AluOpType

P = 128
CHUNK = 256
CHUNKS = B * N // CHUNK
PER_BATCH = N // CHUNK
BANK = 512

SCALED_AT_ONCE_FROM = 3

WARM_UP = 2


def tile_prototypecoefficientsoftcropmasks_kernel(
    tc, f_bytes, f_scale, wp, x, wc, g, box, pix, out
):
    nc = tc.nc
    with ExitStack() as ctx:
        keep = ctx.enter_context(tc.tile_pool(name="keep", bufs=1))
        work = ctx.enter_context(tc.tile_pool(name="work", bufs=3))
        psum = ctx.enter_context(tc.psum_pool(name="psum", bufs=2))
        ctx.enter_context(tc.manual_schedule())

        f_raw = [keep.tile([P, 2 * D], U8, name="f_raw%d" % c, align_bytes=64) for c in range(CHUNKS)]
        wp_raw = keep.tile([P, 4, K], BF16, align_bytes=64)
        wc_raw = keep.tile([P, 4, K], BF16, align_bytes=64)
        x_raw = keep.tile([P, B, D], BF16, align_bytes=64)
        scale_kt = keep.tile([P, 1, 4], F32)
        scale_row = keep.tile([P, D], F32)
        gain_kt = keep.tile([P, 1, 4], BF16)
        box_raw = keep.tile([P, B, 4], BF16)
        pix_rows = keep.tile([P, 512], BF16)
        nc.vector.memset(pix_rows[:], 0.0)

        def load_f(c):
            b, n0 = divmod(c * CHUNK, N)
            nc.sync.dma_start(
                out=f_raw[c][:].rearrange("p (j k) -> p j k", j=2),
                in_=f_bytes[b, n0 : n0 + CHUNK, :].rearrange("(r j) k -> r j k", j=2),
            )

        table = keep.tile([P, 1], F32)
        nc.vector.memset(table[:], 0.0)
        nc.scalar.dma_start(out=scale_kt[:, 0, :], in_=f_scale.rearrange("a b (p t) -> p (a b t)", t=4))
        nc.scalar.dma_start(out=pix_rows[0:4, :], in_=pix.rearrange("(r n) c -> r (n c)", r=4))
        nc.scalar.dma_start(out=box_raw[:], in_=box.rearrange("b q c -> q b c"))
        nc.scalar.dma_start(out=gain_kt[:, 0, :], in_=g.rearrange("(p t) -> p t", t=4))
        nc.scalar.activation(out=table[:], in_=table[:], func=ACT.Sigmoid)
        load_f(0)
        nc.sync.dma_start(out=wp_raw[:], in_=wp.rearrange("(p j) w -> p j w", j=4))
        load_f(1)
        nc.sync.dma_start(out=x_raw[:], in_=x.rearrange("b q k -> q b k"))
        load_f(2)
        nc.sync.dma_start(out=wc_raw[:], in_=wc.rearrange("(p j) w -> p j w", j=4))
        for c in range(3, CHUNKS):
            load_f(c)
        nc.sync.dma_start(out=scale_row[:], in_=f_scale.rearrange("a b k -> (a b k)").partition_broadcast(P))

        zero = keep.tile([P, BANK], BF16)
        nc.vector.memset(zero[:], 0.0)
        warm_bank = psum.tile([P, BANK], F32, name="m_bank")
        for k in range(WARM_UP):
            nc.tensor.matmul(warm_bank[:], lhsT=zero[:, 0:P], rhs=zero[:], start=True, stop=True)
        ident = keep.tile([P, P], F32)
        make_identity(nc, ident[:])
        ident_bf = keep.tile([P, P], BF16)
        nc.vector.tensor_copy(out=ident_bf[:], in_=ident[:])
        box8 = keep.tile([P, B, 4], F32)
        nc.gpsimd.tensor_scalar(box8[:], box_raw[:], 8.0, 0.0, ALU.mult, ALU.add)
        scale_jue = keep.tile([P, 1, 4, 2], F32)
        nc.vector.tensor_copy(
            out=scale_jue[:].rearrange("p a (j u) e -> p (a j) (u e)", j=2),
            in_=scale_kt[:].to_broadcast([P, 2, 4]),
        )

        def quantise(values, codes, scales):
            nc.vector.quantize_mx(out=codes.bitcast(FP8X4), scales=scales, in_=values)

        def multiply(acc, left, left_scales, right, right_scales):
            nc.tensor.matmul_mx(
                out=acc,
                lhsT=left.bitcast(FP8X4),
                lhsT_scale=left_scales,
                rhs=right.bitcast(FP8X4),
                rhs_scale=right_scales,
                start=True,
                stop=True,
            )

        wp_grouped = keep.tile([P, 4 * K], BF16, align_bytes=64)
        wp_codes = keep.tile([P, K], U32, align_bytes=64)
        wp_scales = keep.tile([P, K], U8, align_bytes=64)
        wc_grouped = keep.tile([P, 4 * K], BF16, align_bytes=64)
        wc_codes = keep.tile([P, K], U32, align_bytes=64)
        wc_scales = keep.tile([P, K], U8, align_bytes=64)

        def group_wp(half):
            ts = slice(2 * half, 2 * half + 2)
            nc.vector.tensor_copy(
                out=wp_grouped[:].rearrange("p (t m j) -> p t m j", t=4, j=4)[:, ts],
                in_=wp_raw[:].rearrange("p j (m t) -> p t m j", t=4)[:, ts],
            )

        def group_wc(half):
            for t in (2 * half, 2 * half + 1):
                nc.gpsimd.tensor_scalar(
                    wc_grouped[:].rearrange("p (t m j) -> p t m j", t=4, j=4)[:, t],
                    wc_raw[:].rearrange("p j (m t) -> p t m j", t=4)[:, t],
                    1.0,
                    0.0,
                    ALU.mult,
                    ALU.add,
                )

        wide, turned, f_grouped, f_codes, f_scales = {}, {}, {}, {}, {}
        p_banks, p_grouped, p_codes, p_scales = {}, {}, {}, {}
        m_banks, sigmoids = {}, {}

        def widen(c):
            f_wide = work.tile([P, 2 * D], BF16, bufs=4, align_bytes=64)
            if c < SCALED_AT_ONCE_FROM:
                nc.vector.tensor_copy(out=f_wide[:], in_=f_raw[c][:].bitcast(FP8))
            else:
                for j in range(2):
                    ks = slice(D * j, D * (j + 1))
                    nc.vector.tensor_tensor(
                        out=f_wide[:, ks], in0=f_raw[c][:, ks].bitcast(FP8), in1=scale_row[:], op=ALU.mult
                    )
            wide[c] = f_wide

        def turn(c):
            turn_bank = psum.tile([P, BANK], F32, name="turn_bank")
            words = wide[c][:].bitcast(F32)
            for j in range(2):
                for u in range(2):
                    s = 2 * j + u
                    nc.tensor.transpose(
                        turn_bank[:, P * s : P * (s + 1)], words[:, 256 * j + u : 256 * (j + 1) : 2], ident[:]
                    )
            turned[c] = turn_bank

        def group_f(c):
            f_group = work.tile([P, 4 * CHUNK], BF16, align_bytes=64)
            if c < SCALED_AT_ONCE_FROM:
                nc.vector.tensor_tensor(
                    out=f_group[:].rearrange("p (r s e) -> p r s e", s=4, e=2),
                    in0=turned[c][:].bitcast(BF16).rearrange("p (s r e) -> p r s e", s=4, e=2),
                    in1=scale_jue[:].to_broadcast([P, P, 4, 2]),
                    op=ALU.mult,
                )
            else:
                nc.scalar.copy(
                    out=f_group[:].bitcast(F32).rearrange("p (r s) -> p r s", s=4),
                    in_=turned[c][:].rearrange("p (s r) -> p r s", s=4),
                )
            f_grouped[c] = f_group

        def quantise_f(c):
            f_code = work.tile([P, CHUNK], U32, align_bytes=64)
            f_scl = work.tile([P, CHUNK], U8, align_bytes=64)
            quantise(f_grouped[c][:], f_code[:], f_scl[:])
            f_codes[c], f_scales[c] = f_code, f_scl

        def take_p_banks(c):
            p_banks[c] = []
            for h in range(2):
                p_bank = psum.tile([P, BANK], F32, name="p_bank", bufs=4)
                p_banks[c].append(p_bank)

        def spare(c):
            multiply(p_banks[c][0][:], wp_codes[:, 0:P], wp_scales[:, 0:P], wp_codes[:], wp_scales[:])

        def project(c):
            for h in range(2):
                for t in range(4):
                    ts = slice(P * t, P * (t + 1))
                    ns = slice(P * h, P * (h + 1))
                    multiply(
                        p_banks[c][h][:, ts], wp_codes[:, ts], wp_scales[:, ts], f_codes[c][:, ns], f_scales[c][:, ns]
                    )

        def group_p(c):
            p_group = work.tile([P, 2, BANK], BF16, align_bytes=64)
            for h in range(2):
                copy = nc.vector.tensor_copy if (c, h) == (CHUNKS - 1, 1) else nc.scalar.copy
                copy(
                    out=p_group[:, h, :].rearrange("p (n t) -> p n t", t=4),
                    in_=p_banks[c][h][:].rearrange("p (t n) -> p n t", t=4),
                )
            p_grouped[c] = p_group

        def quantise_p(c):
            p_code = keep.tile([P, CHUNK], U32, name="p_code%d" % c, align_bytes=64)
            p_scl = keep.tile([P, CHUNK], U8, name="p_scl%d" % c, align_bytes=64)
            quantise(p_grouped[c][:].rearrange("p h w -> p (h w)"), p_code[:], p_scl[:])
            p_codes[c], p_scales[c] = p_code, p_scl

        def logits(c):
            pair, half = divmod(c, 2)
            if half == 0:
                m_bank = psum.tile([P, BANK], F32, name="m_bank")
                m_banks[pair] = m_bank
            qs = slice(Q * (c // PER_BATCH), Q * (c // PER_BATCH + 1))
            multiply(
                m_banks[pair][:, CHUNK * half : CHUNK * (half + 1)],
                c_codes[:, qs],
                c_scales[:, qs],
                p_codes[c][:],
                p_scales[c][:],
            )

        def squash(c, count):
            half = c % 2
            sigmoid_m = work.tile([P, CHUNK * count], F32, bufs=7)
            nc.scalar.activation(
                out=sigmoid_m[:],
                in_=m_banks[c // 2][:, CHUNK * half : CHUNK * (half + count)],
                func=ACT.Sigmoid,
                scale=3.0 / sqrt(K),
            )
            sigmoids[c] = sigmoid_m

        def mask(c, count):
            b, n0 = divmod(c * CHUNK, N)
            ns = slice(n0, n0 + CHUNK * count)
            result = work.tile([P, CHUNK * count], F32, bufs=7)
            nc.vector.tensor_mul(result[:], sigmoids[c][:], sides[b][0][:, ns])
            nc.sync.dma_start(out=out[b, :, ns], in_=result[:])

        sides = [[keep.tile([P, N], F32, name="side%d%d" % (b, a)) for a in range(2)] for b in range(B)]
        pix_banks = {}

        def spread_pixels(axis, half):
            pix_bank = psum.tile([P, BANK], F32, name="p_bank", bufs=4)
            for i in range(2):
                r = 2 * half + i
                nc.tensor.matmul(
                    pix_bank[:, 256 * i : 256 * (i + 1)],
                    lhsT=ident_bf[:, r : r + 1].to_broadcast([P, P]),
                    rhs=pix_rows[:, axis::2],
                    start=True,
                    stop=True,
                )
            pix_banks[axis, half] = pix_bank

        def distance(axis, half):
            for b in range(B):
                nc.scalar.activation(
                    out=sides[b][axis][:, BANK * half : BANK * (half + 1)],
                    in_=pix_banks[axis, half][:],
                    func=ACT.Abs,
                    scale=-1.0,
                    bias=box_raw[:, b, axis : axis + 1],
                )

        def side(b, axis):
            nc.scalar.activation(
                out=sides[b][axis][:],
                in_=sides[b][axis][:],
                func=ACT.Sigmoid,
                scale=-8.0,
                bias=box8[:, b, 2 + axis : 3 + axis],
            )

        def crop(b, half):
            ns = slice(BANK * half, BANK * (half + 1))
            nc.vector.tensor_mul(sides[b][0][:, ns], sides[b][0][:, ns], sides[b][1][:, ns])

        x_grouped = keep.tile([P, 4 * B * Q], BF16, align_bytes=64)
        x_codes = keep.tile([P, B * Q], U32, align_bytes=64)
        x_scales = keep.tile([P, B * Q], U8, align_bytes=64)
        tanh_h = keep.tile([P, 4, B * Q], F32)
        c_grouped = keep.tile([P, B, 4 * Q], BF16, align_bytes=64)
        c_codes = keep.tile([P, B * Q], U32, align_bytes=64)
        c_scales = keep.tile([P, B * Q], U8, align_bytes=64)

        def turn_x():
            x_bank = psum.tile([P, BANK], F32, name="turn_bank")
            for b in range(B):
                words = x_raw[:, b, :].bitcast(F32)
                for u in range(2):
                    s = 2 * b + u
                    nc.tensor.transpose(x_bank[:, P * s : P * (s + 1)], words[:, u::2], ident[:])
            return x_bank

        def group_x(x_bank):
            nc.scalar.copy(
                out=x_grouped[:].bitcast(F32).rearrange("p (b q u) -> p b q u", b=B, u=2),
                in_=x_bank[:].rearrange("p (b u q) -> p b q u", b=B, u=2),
            )

        def hidden():
            h_banks = []
            for k in range(2):
                h_bank = psum.tile([P, BANK], F32, name="m_bank")
                for i in range(2):
                    ts = slice(P * (2 * k + i), P * (2 * k + i + 1))
                    multiply(h_bank[:, 256 * i : 256 * (i + 1)], wc_codes[:, ts], wc_scales[:, ts], x_codes[:], x_scales[:])
                h_banks.append(h_bank)
            return h_banks

        def squash_h(h_banks):
            for k in range(2):
                nc.scalar.activation(
                    out=tanh_h[:, 2 * k : 2 * k + 2, :],
                    in_=h_banks[k][:].rearrange("p (t q) -> p t q", t=2),
                    func=ACT.Tanh,
                )

        def gain(b):
            nc.vector.tensor_tensor(
                out=c_grouped[:, b, :].rearrange("p (q t) -> p q t", t=4),
                in0=tanh_h[:, :, Q * b : Q * (b + 1)].rearrange("p t q -> p q t"),
                in1=gain_kt[:].to_broadcast([P, Q, 4]),
                op=ALU.mult,
            )

        widen(0)
        group_wp(0)
        widen(1)
        group_wp(1)
        spread_pixels(0, 0)
        spread_pixels(0, 1)
        spread_pixels(1, 0)
        turn(0)
        spread_pixels(1, 1)
        turn(1)
        x_bank = turn_x()
        for axis in range(2):
            for half in range(2):
                distance(axis, half)
        side(0, 0)
        group_f(0)
        quantise_f(0)
        quantise(wp_grouped[:], wp_codes[:], wp_scales[:])
        take_p_banks(0)
        project(0)

        for i in range(CHUNKS + 1):
            if i + 2 < CHUNKS:
                widen(i + 2)

            if i < 2:
                group_wc(i)
            if i == 1:
                group_x(x_bank)
            if i == 2:
                side(1, 0)
                crop(0, 0)
                h_banks = hidden()
            if i == 3:
                squash_h(h_banks)
            if i == 4:
                logits(0)
                logits(1)
                logits(2)
            if i == 5:
                squash(0, 2)
            if i == 7:
                crop(1, 1)
                logits(4)
                logits(5)
            if i == 8:
                squash(6, 1)

            if i + 1 < CHUNKS:
                group_f(i + 1)
            if i + 2 < CHUNKS:
                turn(i + 2)
            if i + 1 < CHUNKS:
                take_p_banks(i + 1)
                spare(i + 1)

            if i == 0:
                side(0, 1)
            if i == 6:
                squash(2, 2)
            if i >= 1:
                quantise_p(i - 1)
            if i == 3:
                gain(0)
            if i + 1 < CHUNKS:
                quantise_f(i + 1)
            if i == 1:
                quantise(wc_grouped[:], wc_codes[:], wc_scales[:])
                quantise(x_grouped[:], x_codes[:], x_scales[:])
            if i == 3:
                gain(1)
                crop(0, 1)
                quantise(c_grouped[:].rearrange("p b w -> p (b w)"), c_codes[:], c_scales[:])
            if i == 5:
                mask(0, 2)
                crop(1, 0)
            if i == 6:
                mask(2, 2)

            if i < CHUNKS:
                group_p(i)
            if i == 4:
                side(1, 1)
            if i == 5:
                logits(3)
            if i == 7:
                squash(4, 2)
                logits(6)
            if i + 1 < CHUNKS:
                project(i + 1)

        logits(7)
        squash(7, 1)
        mask(4, 2)
        mask(6, 1)
        mask(7, 1)
